import numpy as np
import ml_dtypes


def mxq(x, axis, fmt="e4m3"):
    dtype, down = {"e4m3": (ml_dtypes.float8_e4m3fn, 7), "e5m2": (ml_dtypes.float8_e5m2, 14)}[fmt]
    v = np.moveaxis(np.asarray(x, np.float32).astype(ml_dtypes.bfloat16).astype(np.float64), axis, -1)
    blocks = v.reshape(v.shape[:-1] + (-1, 32))
    amax = np.abs(blocks).max(-1, keepdims=True)
    byte = np.maximum(np.where(amax > 0, np.frexp(amax)[1] - 1 + 127, 0) - down, 1)
    scale = np.exp2(byte - 127.0)
    codes = (blocks / scale).astype(np.float32).astype(dtype).astype(np.float64)
    return np.moveaxis((codes * scale).reshape(v.shape), -1, axis)


WIDE = False


def mx_kscale(k):
    if not WIDE:
        return np.ones(k)
    levels = np.array([10, -10, 5, -5, 0])
    if k % 512:
        return np.exp2(np.random.permutation(np.resize(levels, k // 32))).repeat(32)
    a = np.empty((k // 512, 16))
    for p in range(k // 512):
        a[p, :8] = np.random.permutation(np.resize(levels, 8))
        for g in range(8):
            far = levels[np.abs(levels - a[p, g]) >= 10]
            a[p, g + 8] = far[np.random.randint(len(far))]
    return np.exp2(a.ravel()).repeat(32)


BF16 = ml_dtypes.bfloat16


def bf(x):
    return np.asarray(x, np.float32).astype(BF16)


def f64(x):
    return np.asarray(x).astype(np.float64)

E4M3FN = np.array([(-1.0 if i & 128 else 1.0) * ((1.0 + (i & 7) / 8.0) * 2.0 ** (((i >> 3) & 15) - 7) if i & 120 else (i & 7) * 2.0 ** -9) for i in range(256)])


def e4m3fn_bytes(y):
    return np.clip(np.asarray(y, np.float64), -448.0, 448.0).astype(np.float32).astype(ml_dtypes.float8_e4m3fn).view(np.uint8)


def e4m3fn_values(b):
    return E4M3FN[b]


T, K, N, R, G = 1024, 2048, 1536, 512, 128
FP8_MAX = 448.0


def setup_inputs():
    s, t = mx_kscale(K), mx_kscale(R)
    x = np.random.standard_normal((T, K)) * s
    w = np.random.standard_normal((N, K)) / np.sqrt(K) / s
    x_scale = (np.abs(x).reshape(T, K // G, G).max(axis=2) / FP8_MAX).astype(np.float32)
    w_scale = (np.abs(w).reshape(N // G, G, K // G, G).max(axis=(1, 3)) / FP8_MAX).astype(np.float32)
    x_bytes = e4m3fn_bytes(x / np.repeat(f64(x_scale), G, axis=1))
    w_bytes = e4m3fn_bytes(w / np.repeat(np.repeat(f64(w_scale), G, axis=0), G, axis=1))
    return {"x_bytes": x_bytes, "x_scale": x_scale,
            "w_bytes": w_bytes, "w_scale": w_scale,
            "a": bf(np.random.standard_normal((K, R)) / np.sqrt(K) / s[:, None] * t),
            "lam": bf(1 + 0.1 * np.random.standard_normal(R)),
            "b": bf(np.random.standard_normal((R, N)) / np.sqrt(R) / t[:, None]),
            "c": bf(np.random.uniform(0.5, 1.5, T))}


def reference(x_bytes, x_scale, w_bytes, w_scale, a, lam, b, c):
    x = e4m3fn_values(x_bytes) * np.repeat(f64(x_scale), G, axis=1)
    w = e4m3fn_values(w_bytes) * np.repeat(np.repeat(f64(w_scale), G, axis=0), G, axis=1)
    xq = mxq(x, 1, "e4m3")
    base = xq @ mxq(w, 1, "e4m3").T
    h = (xq @ mxq(f64(a), 0, "e4m3")) * f64(lam)
    d = mxq(h, 1, "e4m3") @ mxq(f64(b), 0, "e4m3")
    return base + f64(c)[:, None] * d

from contextlib import ExitStack

import concourse.mybir as mybir
from concourse.masks import make_identity

T, K, N, R, G = 1024, 2048, 1536, 512, 128
P = 128
FLOPS = 2 * T * K * N + 2 * T * K * R + 2 * T * R * N

F32 = mybir.dt.float32
BF16 = mybir.dt.bfloat16
U32 = mybir.dt.uint32
U8 = mybir.dt.uint8
FP8 = mybir.dt.float8_e4m3fn
FP8X4 = mybir.dt.float8_e4m3fn_x4
MULT = mybir.AluOpType.mult
ADD = mybir.AluOpType.add
COPY = mybir.ActivationFunctionType.Copy

XT = T // P
PASSES = K // 512
CHUNKS = ((0, 512), (512, 512), (1024, 256), (1280, 256))
ORDER = (("x", 0), ("x", 1), ("x", 2), ("x", 3), ("x", 4), ("x", 5), ("x", 6), ("x", 7), ("w", 0), ("w", 1), ("w", 2), ("w", 3))
SBLOCKS = frozenset(((0, 3), (1, 3), (2, 3), (3, 3), (4, 3), (5, 3), (6, 3), (7, 3), (8, 3), (9, 3), (10, 3), (11, 3), (12, 3), (13, 3), (14, 3), (15, 3), (16, 3), (17, 3), (18, 3), (19, 3),))
AIL = "SVSV"
BIL = "SSS"


def tile_fp8_base_lora_d2_kernel(tc, x_bytes, x_scale, w_bytes, w_scale, a, lam, b, c, out):
    nc = tc.nc
    with ExitStack() as ctx:
        const = ctx.enter_context(tc.tile_pool(name="const", bufs=1))
        codes = ctx.enter_context(tc.tile_pool(name="codes", bufs=1))
        xload = ctx.enter_context(tc.tile_pool(name="xload", bufs=8))
        wload = ctx.enter_context(tc.tile_pool(name="wload", bufs=12))
        rload = ctx.enter_context(tc.tile_pool(name="rload", bufs=5))
        widep = ctx.enter_context(tc.tile_pool(name="widep", bufs=3))
        groupp = ctx.enter_context(tc.tile_pool(name="groupp", bufs=3))
        hpool = ctx.enter_context(tc.tile_pool(name="hpool", bufs=3))
        ypool = ctx.enter_context(tc.tile_pool(name="ypool", bufs=1))
        ps_t = ctx.enter_context(tc.psum_pool(name="ps_t", bufs=4))
        ps_h = ctx.enter_context(tc.psum_pool(name="ps_h", bufs=2))
        ps_b = ctx.enter_context(tc.psum_pool(name="ps_b", bufs=2))

        xs = const.tile([P, XT * 16], F32, name="xs")
        nc.sync.dma_start(out=xs[:], in_=x_scale.rearrange("(p m) j -> p (m j)", m=XT))
        x_view = x_bytes.rearrange("(p m) k -> p m k", m=XT)
        a_view = a.rearrange("(g p j) r -> g p j r", p=P, j=4)
        b_view = b.rearrange("(p j) n -> p j n", j=4)
        w_view = w_bytes.rearrange("(r p) k -> r p k", p=P)
        xb, araw, braw, wb = {}, {}, {}, {}

        def load_x(m):
            t = xload.tile([P, K], U8, name="x_b", align_bytes=64)
            nc.sync.dma_start(out=t[:], in_=x_view[:, m, :])
            xb[m] = t

        def load_a(g):
            t = rload.tile([P, 4, 512], BF16, name="ab_raw", align_bytes=64)
            nc.sync.dma_start(out=t[:], in_=a_view[g])
            araw[g] = t

        def load_b(i):
            t = rload.tile([P, 4, 512], BF16, name="ab_raw", align_bytes=64)
            nc.sync.dma_start(out=t[:], in_=b_view[:, :, 512 * i : 512 * (i + 1)])
            braw[i] = t

        def load_w(r):
            t = wload.tile([P, K], U8, name="w_b", align_bytes=64)
            nc.sync.dma_start(out=t[:], in_=w_view[r])
            wb[r] = t

        ident = const.tile([P, P], F32, name="ident")
        make_identity(nc, ident[:])

        lam_b = const.tile([P, 4], BF16, name="lam_b")
        c_b = const.tile([P, XT], BF16, name="c_b")
        ws = const.tile([P, 192], F32, name="ws")
        for what in "x0 a0 a1 lam c x1 a2 a3 x2 x3 ws x4 x5 w0 w1 w2 w3 x6 x7 b0 b1 b2 w4 w5 w6 w7 w8 w9 w10 w11".split(" "):
            if what == "lam":
                nc.sync.dma_start(out=lam_b[:], in_=lam.rearrange("(p t) -> p t", t=4))
            elif what == "c":
                nc.sync.dma_start(out=c_b[:], in_=c.rearrange("(p m) -> p m", m=XT))
            elif what == "ws":
                nc.sync.dma_start(out=ws[:], in_=w_scale.rearrange("i j -> (i j)").partition_broadcast(P))
            elif what[0] == "x":
                load_x(int(what[1:]))
            elif what[0] == "a":
                load_a(int(what[1:]))
            elif what[0] == "b":
                load_b(int(what[1:]))
            else:
                load_w(int(what[1:]))

        lam_f = const.tile([P, 4], F32, name="lam_f")
        nc.scalar.activation(out=lam_f[:], in_=lam_b[:], func=COPY)
        c_f = const.tile([P, XT], F32, name="c_f")
        nc.scalar.activation(out=c_f[:], in_=c_b[:], func=COPY)

        units = []
        x_unit, w_unit = {}, {}
        for kind, idx in ORDER:
            if kind == "x":
                x_unit[idx] = len(units)
                units.append([("x", idx, g) for g in range(PASSES)])
            else:
                n0, rows = CHUNKS[idx]
                w_unit[idx] = len(units)
                blocks = [("w", n0 // P + r, g) for g in range(PASSES) for r in range(rows // P)]
                units.extend([blocks[i : i + 4] for i in range(0, len(blocks), 4)])
        SLOTS = len(units)
        wide = {}
        grouped = {}
        ucodes = {}
        uscales = {}

        def widen(s):
            wide[s] = widep.tile([P, 4, 2, P, 2], BF16, name="wide", align_bytes=64)
            for i, (kind, row, g) in enumerate(units[s]):
                src = xb[row] if kind == "x" else wb[row]
                sc = xs if kind == "x" else ws
                if (s, i) in SBLOCKS:
                    flat = wide[s][:, i, :, :, :].rearrange("p u w e -> p (u w e)")
                    for q in range(4):
                        k0 = 512 * g + P * q
                        j = 16 * row + 4 * g + q
                        nc.scalar.activation(
                            out=flat[:, P * q : P * (q + 1)], in_=src[:, k0 : k0 + P].bitcast(FP8), func=COPY, scale=sc[:, j : j + 1]
                        )
                    continue
                for q in range(4):
                    k0 = 512 * g + P * q
                    j = 16 * row + 4 * g + q
                    nc.vector.tensor_scalar(
                        out=wide[s][:, i, :, 32 * q : 32 * (q + 1), :].rearrange("p u w e -> p w u e"),
                        in0=src[:, k0 : k0 + P].bitcast(FP8).rearrange("p (w u e) -> p w u e", u=2, e=2),
                        scalar1=sc[:, j : j + 1],
                        scalar2=None,
                        op0=MULT,
                    )

        def turn(s):
            grouped[s] = groupp.tile([P, 4, P, 4], BF16, name="grouped", align_bytes=64)
            for h in range(2):
                xt = ps_t.tile([P, 4, P], F32, name="xt")
                for i in range(2):
                    for u in range(2):
                        if (s, 2 * h + i) in SBLOCKS:
                            words = wide[s][:, 2 * h + i, :, :, :].rearrange("p u w e -> p (u w e)").bitcast(F32)[:, u :: 2]
                        else:
                            words = wide[s][:, 2 * h + i, u, :, :].rearrange("p w e -> p (w e)").bitcast(F32)
                        nc.tensor.transpose(xt[:, 2 * i + u, :], words, ident[:])
                nc.scalar.copy(
                    out=grouped[s][:, 2 * h : 2 * h + 2, :, :].rearrange("p i w t -> p (i w t)").bitcast(F32).rearrange("p (i w u) -> p i w u", i=2, u=2),
                    in_=xt[:].rearrange("p (i u) w -> p i w u", u=2),
                )

        def quant(s):
            ucodes[s] = codes.tile([P, 512], U32, name="codes%d" % s, align_bytes=64)
            uscales[s] = codes.tile([P, 512], U8, name="scales%d" % s, align_bytes=64)
            nc.vector.quantize_mx(
                out=ucodes[s][:].bitcast(FP8X4), scales=uscales[s][:], in_=grouped[s][:].rearrange("p i w t -> p (i w t)")
            )

        a_int, a_codes, a_scales = {}, {}, {}
        b_int, b_codes, b_scales = {}, {}, {}

        def inter_a(g, eng):
            a_int[g] = groupp.tile([P, 4, P, 4], BF16, name="ab_int", align_bytes=64)
            (nc.scalar.copy if eng == "S" else nc.vector.tensor_copy)(
                out=a_int[g][:], in_=araw[g][:].rearrange("p j (m t) -> p t m j", t=4)
            )

        def quant_a(g):
            a_codes[g] = codes.tile([P, 512], U32, name="acodes%d" % g, align_bytes=64)
            a_scales[g] = codes.tile([P, 512], U8, name="ascales%d" % g, align_bytes=64)
            nc.vector.quantize_mx(
                out=a_codes[g][:].bitcast(FP8X4), scales=a_scales[g][:], in_=a_int[g][:].rearrange("p t m j -> p (t m j)")
            )

        def inter_b(i, eng):
            b_int[i] = groupp.tile([P, 4, P, 4], BF16, name="ab_int", align_bytes=64)
            (nc.scalar.copy if eng == "S" else nc.vector.tensor_copy)(
                out=b_int[i][:].rearrange("p t m j -> p (t m) j"), in_=braw[i][:].rearrange("p j n -> p n j")
            )

        def quant_b(i):
            b_codes[i] = codes.tile([P, 512], U32, name="bcodes%d" % i, align_bytes=64)
            b_scales[i] = codes.tile([P, 512], U8, name="bscales%d" % i, align_bytes=64)
            nc.vector.quantize_mx(
                out=b_codes[i][:].bitcast(FP8X4), scales=b_scales[i][:], in_=b_int[i][:].rearrange("p t m j -> p (t m j)")
            )

        hps, hg, h_codes, h_scales = {}, {}, {}, {}

        def down(m):
            hps[m] = ps_h.tile([P, 4, P], F32, name="hd")
            for t in range(4):
                for g in range(PASSES):
                    nc.tensor.matmul_mx(
                        out=hps[m][:, t, :],
                        lhsT=a_codes[g][:, P * t : P * (t + 1)].bitcast(FP8X4),
                        lhsT_scale=a_scales[g][:, P * t : P * (t + 1)],
                        rhs=ucodes[x_unit[m]][:, P * g : P * (g + 1)].bitcast(FP8X4),
                        rhs_scale=uscales[x_unit[m]][:, P * g : P * (g + 1)],
                        start=(g == 0),
                        stop=(g == PASSES - 1),
                    )

        def scale_h(m):
            hg[m] = hpool.tile([P, P, 4], BF16, name="h_grouped", align_bytes=64)
            nc.vector.tensor_tensor(
                out=hg[m][:],
                in0=hps[m][:].rearrange("p t w -> p w t"),
                in1=lam_f[:].unsqueeze(1).to_broadcast([P, P, 4]),
                op=MULT,
            )

        def quant_h(m):
            h_codes[m] = codes.tile([P, P], U32, name="hcodes%d" % m, align_bytes=64)
            h_scales[m] = codes.tile([P, P], U8, name="hscales%d" % m, align_bytes=64)
            nc.vector.quantize_mx(
                out=h_codes[m][:].bitcast(FP8X4), scales=h_scales[m][:], in_=hg[m][:].rearrange("p w t -> p (w t)")
            )

        y = {}
        dps = {}

        def up(m, i):
            ps = ps_h.tile([P, 512], F32, name="hd")
            nc.tensor.matmul_mx(
                out=ps[:],
                lhsT=h_codes[m][:].bitcast(FP8X4),
                lhsT_scale=h_scales[m][:],
                rhs=b_codes[i][:].bitcast(FP8X4),
                rhs_scale=b_scales[i][:],
                start=True,
                stop=True,
            )
            y[m, i] = ypool.tile([P, 512], F32, name="y%d_%d" % (m, i), align_bytes=64)
            nc.scalar.activation(out=y[m, i][:], in_=ps[:], func=COPY, scale=c_f[:, m : m + 1])

        out_view = out.rearrange("(p m) n -> p m n", m=XT)
        bps = {}

        def base(m, ci):
            n0, rows = CHUNKS[ci]
            first = w_unit[ci]
            ps = ps_b.tile([P, 512], F32, name="base")
            bps[m, ci] = ps
            for g in range(PASSES):
                blk = g * (rows // P)
                s, c0 = first + blk // 4, P * (blk % 4)
                nc.tensor.matmul_mx(
                    out=ps[:, :rows],
                    lhsT=ucodes[x_unit[m]][:, P * g : P * (g + 1)].bitcast(FP8X4),
                    lhsT_scale=uscales[x_unit[m]][:, P * g : P * (g + 1)],
                    rhs=ucodes[s][:, c0 : c0 + rows].bitcast(FP8X4),
                    rhs_scale=uscales[s][:, c0 : c0 + rows],
                    start=(g == 0),
                    stop=(g == PASSES - 1),
                )

        def finish(m, ci):
            n0, rows = CHUNKS[ci]
            yt = y[m, n0 // 512][:, n0 % 512 : n0 % 512 + rows]
            nc.vector.tensor_tensor(out=yt, in0=bps[m, ci][:, :rows], in1=yt, op=ADD)
            nc.sync.dma_start(out=out_view[:, m, n0 : n0 + rows], in_=yt)

        jobs = {}

        def at(s, fn, *args):
            jobs.setdefault(s, []).append((fn, args))

        for g in range(4):
            at(g, inter_a, g, AIL[g])
            at(g + 1, quant_a, g)
        for i in range(3):
            at(6 + i, inter_b, i, BIL[i])
            at(6 + 2 + i, quant_b, i)
        ready_h = {}
        for m in range(XT):
            s = max(x_unit[m] + 3, 5 + (m + 1) // 2)
            at(s, down, m)
            at(s + 1, scale_h, m)
            at(s + 2, quant_h, m)
            ready_h[m] = s + 2
        ready_u = {}
        load = {}
        todo = []
        for ci in range(len(CHUNKS)):
            w_ready = w_unit[ci] + CHUNKS[ci][1] // P - 1 + 3
            for m in range(XT):
                todo.append((max(w_ready, x_unit[m] + 3), ci, m))
        todo = sorted(todo)
        for s, ci, m in todo:
            i = CHUNKS[ci][0] // 512
            s = max(s, ready_h[m] + 2, 6 + 4 + i + 1)
            cost = CHUNKS[ci][1] // 256
            while load.get(s, 0) + cost > 6:
                s += 1
            load[s] = load.get(s, 0) + cost
            if (m, i) not in ready_u:
                ready_u[m, i] = s
                at(s - 1, up, m, i)
            at(s, base, m, ci)
            at(s, finish, m, ci)
        last = max(jobs)
        for s in range(last + 1):
            if s < SLOTS:
                widen(s)
            if 0 <= s - 2 < SLOTS:
                quant(s - 2)
            if 0 <= s - 1 < SLOTS:
                turn(s - 1)
            for fn, args in jobs.get(s, []):
                if fn == up:
                    fn(*args)
            for fn, args in jobs.get(s, []):
                if fn != up:
                    fn(*args)
